import numpy as np
import ml_dtypes


def mxq(x, axis, fmt="e4m3"):
    dtype, down = {"e4m3": (ml_dtypes.float8_e4m3fn, 7), "e5m2": (ml_dtypes.float8_e5m2, 14)}[fmt]
    v = np.moveaxis(np.asarray(x, np.float32).astype(ml_dtypes.bfloat16).astype(np.float64), axis, -1)
    blocks = v.reshape(v.shape[:-1] + (-1, 32))
    amax = np.abs(blocks).max(-1, keepdims=True)
    byte = np.maximum(np.where(amax > 0, np.frexp(amax)[1] - 1 + 127, 0) - down, 1)
    scale = np.exp2(byte - 127.0)
    codes = (blocks / scale).astype(np.float32).astype(dtype).astype(np.float64)
    return np.moveaxis((codes * scale).reshape(v.shape), -1, axis)


WIDE = False


def mx_kscale(k):
    if not WIDE:
        return np.ones(k)
    levels = np.array([10, -10, 5, -5, 0])
    if k % 512:
        return np.exp2(np.random.permutation(np.resize(levels, k // 32))).repeat(32)
    a = np.empty((k // 512, 16))
    for p in range(k // 512):
        a[p, :8] = np.random.permutation(np.resize(levels, 8))
        for g in range(8):
            far = levels[np.abs(levels - a[p, g]) >= 10]
            a[p, g + 8] = far[np.random.randint(len(far))]
    return np.exp2(a.ravel()).repeat(32)


def f64(x):
    return np.asarray(x).astype(np.float64)


def striped8(idx):
    return np.concatenate([x.reshape(-1, 16).T for x in idx]).astype(np.uint16)


def runs(offs, k):
    lists = np.stack([offs[16 * r : 16 * r + 16].T.reshape(-1) for r in range(8)]).astype(np.int64)
    return lists[np.arange(k) % 512 // 64]


def pack_weight(w):
    k, n = w.shape
    w = f64(np.asarray(w, np.float32).astype(ml_dtypes.bfloat16)).reshape(k // 32, 32, n)
    amax = np.abs(w).max(1)
    byte = np.clip(np.where(amax > 0, np.frexp(amax)[1] - 1 + 127 - 7, 1), 1, 254)
    scaled = (w * np.exp2(127.0 - byte)[:, None, :]).reshape(k, n).astype(np.float32)
    words = np.ascontiguousarray(scaled.reshape(k // 512, 128, 4, n).transpose(0, 1, 3, 2)).astype(ml_dtypes.float8_e4m3fn).view(np.uint8)
    return words, np.ascontiguousarray(byte.astype(np.uint8).reshape(k // 512, 16, n))


def unpack_weight(words, scales):
    g, p, n, _ = words.shape
    vals = np.ascontiguousarray(words).view(ml_dtypes.float8_e4m3fn).astype(np.float64) * np.repeat(np.exp2(scales.astype(np.float64) - 127.0), 8, axis=1)[..., None]
    return vals.transpose(0, 1, 3, 2).reshape(g * 512, n)


def relu(v):
    return np.maximum(v, 0.0)


K, T, S, N, H = 512, 2048, 512, 512, 512


def setup_inputs():
    n = np.random.standard_normal
    s = mx_kscale(K)[:, None]
    u = mx_kscale(H)
    packed_xT = pack_weight(n((K, T)) * s)
    return {
        "x_words": packed_xT[0],
        "x_scales": packed_xT[1],
        "w1": (n((K, H)) / np.sqrt(K) / s * u).astype(np.float32),
        "w2": (n((H, N)) / np.sqrt(H) / u[:, None]).astype(np.float32),
        "offs": striped8(np.stack([np.random.permutation(T)[:S] for _ in range(8)])),
        "back": striped8(np.stack([np.random.permutation(S) for _ in range(8)])),
    }


def reference(x_words, x_scales, w1, w2, offs, back):
    xq = unpack_weight(x_words, x_scales)[np.arange(K)[:, None], runs(offs, K)]
    y = mxq(f64(w1), 0, "e4m3").T @ xq
    z = relu(y[np.arange(H)[:, None], runs(back, H)])
    return mxq(f64(w2), 0, "e4m3").T @ mxq(z, 0, "e4m3")

@@ -1,0 +1,173 @@
+from contextlib import ExitStack
+
+import concourse.mybir as mybir
+
+K, T, S, N, H = 512, 2048, 512, 512, 512
+FLOPS = 2 * K * H * S + 2 * H * N * S
+
+F32 = mybir.dt.float32
+BF16 = mybir.dt.bfloat16
+I32 = mybir.dt.int32
+U32 = mybir.dt.uint32
+U16 = mybir.dt.uint16
+U8 = mybir.dt.uint8
+FP8X4 = mybir.dt.float8_e4m3fn_x4
+RELU = mybir.ActivationFunctionType.Relu
+
+P = 128
+PACK = 4
+LIST_ROWS = 16
+PIECES = (256, 128, 128)
+W1_CHUNKS = 2
+W2_CHUNKS = 2
+W1_VECTOR_M = 40
+
+
+def tile_picked_permun_relu_p_kernel(tc, x_words, x_scales, w1, w2, offs, back, out):
+    nc = tc.nc
+    with ExitStack() as ctx:
+        keep = ctx.enter_context(tc.tile_pool(name="keep", bufs=1))
+        psum = ctx.enter_context(tc.psum_pool(name="psum", bufs=1))
+
+        offs_sb = keep.tile([P, S // LIST_ROWS], U16, name="offs_sb")
+        back_sb = keep.tile([P, S // LIST_ROWS], U16, name="back_sb")
+        word_table = keep.tile([P, T], U32, name="word_table", align_bytes=64)
+        scale_table = keep.tile([P, T], U8, name="scale_table", align_bytes=64)
+
+        nc.vector.memset(scale_table[:].bitcast(I32), 0)
+        nc.sync.dma_start(offs_sb[:], offs)
+        nc.scalar.dma_start(scale_table[0:P:8, :].bitcast(I32), x_scales[0].bitcast(I32))
+        zero_in = keep.tile([P, 1], F32, name="zero_in")
+        nc.vector.memset(zero_in[:], 0.0)
+        zero_bias = keep.tile([P, 1], F32, name="zero_bias", tag="after_relu", align_bytes=64)
+        nc.scalar.activation(zero_bias[:], zero_in[:], RELU)
+        nc.sync.dma_start(word_table[:].bitcast(I32), x_words[0].rearrange("p n r -> p (n r)").bitcast(I32))
+
+        w1_rows = w1.rearrange("(p j) c -> p j c", j=PACK)
+        w1_width = H // W1_CHUNKS
+        w1_raw = []
+        for h in range(W1_CHUNKS):
+            raw = keep.tile([P, PACK, w1_width], F32, name="w1_raw%d" % h)
+            nc.sync.dma_start(raw[:], w1_rows[:, :, h * w1_width : (h + 1) * w1_width])
+            w1_raw.append(raw)
+        nc.sync.dma_start(back_sb[:], back)
+        w2_rows = w2.rearrange("(p j) c -> p j c", j=PACK)
+        w2_width = N // W2_CHUNKS
+        w2_raw = []
+        for h in range(W2_CHUNKS):
+            raw = keep.tile([P, PACK, w2_width], F32, name="w2_raw%d" % h)
+            nc.sync.dma_start(raw[:], w2_rows[:, :, h * w2_width : (h + 1) * w2_width])
+            w2_raw.append(raw)
+
+        picked_scales = keep.tile([P, S], U8, name="picked_scales", align_bytes=64)
+        nc.vector.tensor_copy(picked_scales[:], scale_table[:].indirect(offs_sb[:]))
+        x_plane = keep.tile([P, S], U8, name="x_plane", align_bytes=64)
+        nc.vector.tensor_copy(x_plane[:].bitcast(I32), picked_scales[:].bitcast(I32))
+        for j in range(1, 4):
+            nc.scalar.dma_start(x_plane[j:P:32, :].bitcast(I32), picked_scales[8 * j : P : 32, :].bitcast(I32))
+
+        x_codes = keep.tile([P, S], U32, name="x_codes", align_bytes=64)
+        nc.vector.tensor_copy(x_codes[:], word_table[:].indirect(offs_sb[:]))
+
+        w1_grouped = keep.tile([P, PACK, P, PACK], BF16, name="w1_grouped", tag="after_w1_quantize", align_bytes=64)
+        m_chunk = w1_width // PACK
+        for h in range(W1_CHUNKS):
+            src = w1_raw[h][:].rearrange("p j (m t) -> p m t j", t=PACK)
+            dst = w1_grouped[:, :, h * m_chunk : (h + 1) * m_chunk, :].rearrange("p t m j -> p m t j")
+            nc.vector.tensor_copy(dst[:, :W1_VECTOR_M], src[:, :W1_VECTOR_M])
+            nc.scalar.copy(dst[:, W1_VECTOR_M:], src[:, W1_VECTOR_M:])
+        w1_codes = keep.tile([P, H], U32, name="w1_codes", align_bytes=64)
+        w1_scales = keep.tile([P, H], U8, name="w1_scales", tag="after_first_product", align_bytes=64)
+        for t0, t1 in ((0, 1), (1, 2), (2, 4)):
+            nc.vector.quantize_mx(
+                out=w1_codes[:, t0 * P : t1 * P].bitcast(FP8X4),
+                scales=w1_scales[:, t0 * P : t1 * P],
+                in_=w1_grouped[:, t0:t1].rearrange("p t m j -> p (t m j)"),
+            )
+
+        y_planes = []
+        for t in range(PACK):
+            acc = psum.tile([P, S], F32, name="y_acc%d" % t)
+            nc.tensor.matmul_mx(
+                out=acc[:],
+                lhsT=w1_codes[:, t * P : (t + 1) * P].bitcast(FP8X4),
+                lhsT_scale=w1_scales[:, t * P : (t + 1) * P],
+                rhs=x_codes[:].bitcast(FP8X4),
+                rhs_scale=x_plane[:],
+                start=True,
+                stop=True,
+            )
+            y_plane = keep.tile([P, S], F32, name="y_plane%d" % t)
+            nc.scalar.activation(y_plane[:], acc[:], RELU, bias=zero_bias[:])
+            y_planes.append(y_plane)
+
+        w2_codes = keep.tile([P, N], U32, name="w2_codes", align_bytes=64)
+        w2_scales = keep.tile([P, N], U8, name="w2_scales", align_bytes=64)
+
+        def cast_w2(h):
+            grouped = keep.tile([P, w2_width, PACK], BF16, name="w2_grouped%d" % h, tag=("after_w1_quantize", "after_first_product")[h], align_bytes=64)
+            src = w2_raw[h][:].rearrange("p j c -> p c j")
+            if h == 0:
+                nc.vector.tensor_copy(grouped[:], src)
+            else:
+                nc.scalar.copy(grouped[:], src)
+            return grouped
+
+        def quantize_w2(h, grouped):
+            cols = slice(h * w2_width, (h + 1) * w2_width)
+            nc.vector.quantize_mx(
+                out=w2_codes[:, cols].bitcast(FP8X4), scales=w2_scales[:, cols], in_=grouped[:].rearrange("p c j -> p (c j)")
+            )
+
+        quantize_w2(0, cast_w2(0))
+        w2_second = cast_w2(1)
+
+        out_rows = out.rearrange("(b p) j -> p b j", p=P)
+        starts = [sum(PIECES[:i]) for i in range(len(PIECES))]
+        last = len(PIECES) - 1
+
+        def gather_piece(i):
+            n, j0 = PIECES[i], starts[i]
+            planes = keep.tile([P, PACK, n], BF16, name="z_planes%d" % i, tag=("z_planes0", "after_relu", "after_z_quantize")[i], align_bytes=64)
+            for t in range(PACK):
+                nc.vector.tensor_copy(planes[:, t, :], y_planes[t][:].indirect(back_sb[:, j0 // LIST_ROWS : (j0 + n) // LIST_ROWS]))
+            grouped = keep.tile([P, n, PACK], BF16, name="z_grouped%d" % i, tag=("after_z_quantize", "z_grouped1", "z_grouped2")[i], align_bytes=64)
+            src = planes[:].rearrange("p t n -> p n t")
+            if i == last:
+                nc.vector.tensor_copy(grouped[:], src)
+            else:
+                nc.scalar.copy(grouped[:], src)
+            return grouped
+
+        def finish_piece(i, grouped):
+            n, j0 = PIECES[i], starts[i]
+            z_codes = keep.tile([P, n], U32, name="z_codes%d" % i, align_bytes=64)
+            z_scales = keep.tile([P, n], U8, name="z_scales%d" % i, align_bytes=64)
+            nc.vector.quantize_mx(out=z_codes[:].bitcast(FP8X4), scales=z_scales[:], in_=grouped[:].rearrange("p n t -> p (n t)"))
+            for half in range(2):
+                acc = psum.tile([P, 2, n], F32, name="out_acc", tag="out_acc", bufs=4)
+                for b in range(2):
+                    m_cols = slice((2 * half + b) * P, (2 * half + b + 1) * P)
+                    nc.tensor.matmul_mx(
+                        out=acc[:, b, :],
+                        lhsT=w2_codes[:, m_cols].bitcast(FP8X4),
+                        lhsT_scale=w2_scales[:, m_cols],
+                        rhs=z_codes[:].bitcast(FP8X4),
+                        rhs_scale=z_scales[:],
+                        start=True,
+                        stop=True,
+                    )
+                staged = keep.tile([P, 2, n], F32, name="staged%d_%d" % (i, half))
+                if i == last and half == 1:
+                    nc.vector.tensor_copy(staged[:], acc[:])
+                else:
+                    nc.scalar.copy(staged[:], acc[:])
+                nc.sync.dma_start(out_rows[:, 2 * half : 2 * half + 2, j0 : j0 + n], staged[:])
+
+        pending = gather_piece(0)
+        quantize_w2(1, w2_second)
+        for i in range(1, len(PIECES)):
+            following = gather_piece(i)
+            finish_piece(i - 1, pending)
+            pending = following
+        finish_piece(last, pending)

@@ -20,7 +20,7 @@ LIST_ROWS = 16
 PIECES = (256, 128, 128)
 W1_CHUNKS = 2
 W2_CHUNKS = 2
-W1_VECTOR_M = 40
+WORDS_AHEAD = 512
 
 
 def tile_picked_permun_relu_p_kernel(tc, x_words, x_scales, w1, w2, offs, back, out):
@@ -31,17 +31,19 @@ def tile_picked_permun_relu_p_kernel(tc, x_words, x_scales, w1, w2, offs, back, 
 
         offs_sb = keep.tile([P, S // LIST_ROWS], U16, name="offs_sb")
         back_sb = keep.tile([P, S // LIST_ROWS], U16, name="back_sb")
-        word_table = keep.tile([P, T], U32, name="word_table", align_bytes=64)
-        scale_table = keep.tile([P, T], U8, name="scale_table", align_bytes=64)
+        scale_table = keep.tile([P, T], U8, name="scale_table", tag="after_scale_gather", align_bytes=64)
 
+        word_table = keep.tile([P, T], U32, name="word_table", align_bytes=64)
+        words = x_words[0].rearrange("p n r -> p (n r)").bitcast(I32)
         nc.vector.memset(scale_table[:].bitcast(I32), 0)
         nc.sync.dma_start(offs_sb[:], offs)
-        nc.scalar.dma_start(scale_table[0:P:8, :].bitcast(I32), x_scales[0].bitcast(I32))
+        nc.sync.dma_start(word_table[:, :WORDS_AHEAD].bitcast(I32), words[:, :WORDS_AHEAD])
+        nc.sync.dma_start(scale_table[0:P:8, :].bitcast(I32), x_scales[0].bitcast(I32))
+        nc.sync.dma_start(word_table[:, WORDS_AHEAD:].bitcast(I32), words[:, WORDS_AHEAD:])
         zero_in = keep.tile([P, 1], F32, name="zero_in")
         nc.vector.memset(zero_in[:], 0.0)
         zero_bias = keep.tile([P, 1], F32, name="zero_bias", tag="after_relu", align_bytes=64)
         nc.scalar.activation(zero_bias[:], zero_in[:], RELU)
-        nc.sync.dma_start(word_table[:].bitcast(I32), x_words[0].rearrange("p n r -> p (n r)").bitcast(I32))
 
         w1_rows = w1.rearrange("(p j) c -> p j c", j=PACK)
         w1_width = H // W1_CHUNKS
@@ -51,38 +53,39 @@ def tile_picked_permun_relu_p_kernel(tc, x_words, x_scales, w1, w2, offs, back, 
             nc.sync.dma_start(raw[:], w1_rows[:, :, h * w1_width : (h + 1) * w1_width])
             w1_raw.append(raw)
         nc.sync.dma_start(back_sb[:], back)
-        w2_rows = w2.rearrange("(p j) c -> p j c", j=PACK)
-        w2_width = N // W2_CHUNKS
-        w2_raw = []
-        for h in range(W2_CHUNKS):
-            raw = keep.tile([P, PACK, w2_width], F32, name="w2_raw%d" % h)
-            nc.sync.dma_start(raw[:], w2_rows[:, :, h * w2_width : (h + 1) * w2_width])
-            w2_raw.append(raw)
-
         picked_scales = keep.tile([P, S], U8, name="picked_scales", align_bytes=64)
         nc.vector.tensor_copy(picked_scales[:], scale_table[:].indirect(offs_sb[:]))
         x_plane = keep.tile([P, S], U8, name="x_plane", align_bytes=64)
-        nc.vector.tensor_copy(x_plane[:].bitcast(I32), picked_scales[:].bitcast(I32))
-        for j in range(1, 4):
-            nc.scalar.dma_start(x_plane[j:P:32, :].bitcast(I32), picked_scales[8 * j : P : 32, :].bitcast(I32))
+        nc.gpsimd.memset(x_plane[:].bitcast(I32), 0)
+        for j in range(4):
+            nc.sync.dma_start(x_plane[j:P:32, :].bitcast(I32), picked_scales[8 * j : P : 32, :].bitcast(I32))
+        w2_rows = w2.rearrange("(p j) c -> p j c", j=PACK)
+        w2_width = N // W2_CHUNKS
+        w2_raw = keep.tile([P, W2_CHUNKS, PACK, w2_width], F32, name="w2_raw", tag="after_scale_gather", align_bytes=64)
+        for h in range(W2_CHUNKS):
+            nc.sync.dma_start(w2_raw[:, h], w2_rows[:, :, h * w2_width : (h + 1) * w2_width])
+
 
         x_codes = keep.tile([P, S], U32, name="x_codes", align_bytes=64)
         nc.vector.tensor_copy(x_codes[:], word_table[:].indirect(offs_sb[:]))
 
-        w1_grouped = keep.tile([P, PACK, P, PACK], BF16, name="w1_grouped", tag="after_w1_quantize", align_bytes=64)
+        w1_low = keep.tile([P, 2, P, PACK], BF16, name="w1_low", align_bytes=64)
+        w1_high = keep.tile([P, 2, P, PACK], BF16, name="w1_high", tag="after_w1_quantize", align_bytes=64)
         m_chunk = w1_width // PACK
         for h in range(W1_CHUNKS):
             src = w1_raw[h][:].rearrange("p j (m t) -> p m t j", t=PACK)
-            dst = w1_grouped[:, :, h * m_chunk : (h + 1) * m_chunk, :].rearrange("p t m j -> p m t j")
-            nc.vector.tensor_copy(dst[:, :W1_VECTOR_M], src[:, :W1_VECTOR_M])
-            nc.scalar.copy(dst[:, W1_VECTOR_M:], src[:, W1_VECTOR_M:])
+            m_cols = slice(h * m_chunk, (h + 1) * m_chunk)
+            low = w1_low[:, :, m_cols, :].rearrange("p t m j -> p m t j")
+            high = w1_high[:, :, m_cols, :].rearrange("p t m j -> p m t j")
+            nc.vector.tensor_copy(low, src[:, :, 0:2, :])
+            nc.scalar.copy(high, src[:, :, 2:4, :])
         w1_codes = keep.tile([P, H], U32, name="w1_codes", align_bytes=64)
         w1_scales = keep.tile([P, H], U8, name="w1_scales", tag="after_first_product", align_bytes=64)
-        for t0, t1 in ((0, 1), (1, 2), (2, 4)):
+        for t0, t1, grouped in ((0, 1, w1_low[:, 0:1]), (1, 2, w1_low[:, 1:2]), (2, 4, w1_high[:])):
             nc.vector.quantize_mx(
                 out=w1_codes[:, t0 * P : t1 * P].bitcast(FP8X4),
                 scales=w1_scales[:, t0 * P : t1 * P],
-                in_=w1_grouped[:, t0:t1].rearrange("p t m j -> p (t m j)"),
+                in_=grouped.rearrange("p t m j -> p (t m j)"),
             )
 
         y_planes = []
@@ -106,7 +109,7 @@ def tile_picked_permun_relu_p_kernel(tc, x_words, x_scales, w1, w2, offs, back, 
 
         def cast_w2(h):
             grouped = keep.tile([P, w2_width, PACK], BF16, name="w2_grouped%d" % h, tag=("after_w1_quantize", "after_first_product")[h], align_bytes=64)
-            src = w2_raw[h][:].rearrange("p j c -> p c j")
+            src = w2_raw[:, h].rearrange("p j c -> p c j")
             if h == 0:
                 nc.vector.tensor_copy(grouped[:], src)
             else:
@@ -131,7 +134,7 @@ def tile_picked_permun_relu_p_kernel(tc, x_words, x_scales, w1, w2, offs, back, 
             planes = keep.tile([P, PACK, n], BF16, name="z_planes%d" % i, tag=("z_planes0", "after_relu", "after_z_quantize")[i], align_bytes=64)
             for t in range(PACK):
                 nc.vector.tensor_copy(planes[:, t, :], y_planes[t][:].indirect(back_sb[:, j0 // LIST_ROWS : (j0 + n) // LIST_ROWS]))
-            grouped = keep.tile([P, n, PACK], BF16, name="z_grouped%d" % i, tag=("after_z_quantize", "z_grouped1", "z_grouped2")[i], align_bytes=64)
+            grouped = keep.tile([P, n, PACK], BF16, name="z_grouped%d" % i, tag=("after_z_quantize", "z_grouped_late", "z_grouped_late")[i], align_bytes=64)
             src = planes[:].rearrange("p t n -> p n t")
             if i == last:
                 nc.vector.tensor_copy(grouped[:], src)

@@ -18,7 +18,7 @@ P = 128
 PACK = 4
 LIST_ROWS = 16
 PIECES = (256, 128, 128)
-W1_CHUNKS = 2
+W1_CHUNKS = 1
 W2_CHUNKS = 2
 WORDS_AHEAD = 512
 
@@ -56,7 +56,7 @@ def tile_picked_permun_relu_p_kernel(tc, x_words, x_scales, w1, w2, offs, back, 
         picked_scales = keep.tile([P, S], U8, name="picked_scales", align_bytes=64)
         nc.vector.tensor_copy(picked_scales[:], scale_table[:].indirect(offs_sb[:]))
         x_plane = keep.tile([P, S], U8, name="x_plane", align_bytes=64)
-        nc.gpsimd.memset(x_plane[:].bitcast(I32), 0)
+        nc.vector.memset(x_plane[:].bitcast(I32), 0)
         for j in range(4):
             nc.sync.dma_start(x_plane[j:P:32, :].bitcast(I32), picked_scales[8 * j : P : 32, :].bitcast(I32))
         w2_rows = w2.rearrange("(p j) c -> p j c", j=PACK)
@@ -73,12 +73,12 @@ def tile_picked_permun_relu_p_kernel(tc, x_words, x_scales, w1, w2, offs, back, 
         w1_high = keep.tile([P, 2, P, PACK], BF16, name="w1_high", tag="after_w1_quantize", align_bytes=64)
         m_chunk = w1_width // PACK
         for h in range(W1_CHUNKS):
-            src = w1_raw[h][:].rearrange("p j (m t) -> p m t j", t=PACK)
+            src = w1_raw[h][:].rearrange("p j (m t) -> p m j t", t=PACK)
             m_cols = slice(h * m_chunk, (h + 1) * m_chunk)
-            low = w1_low[:, :, m_cols, :].rearrange("p t m j -> p m t j")
-            high = w1_high[:, :, m_cols, :].rearrange("p t m j -> p m t j")
-            nc.vector.tensor_copy(low, src[:, :, 0:2, :])
-            nc.scalar.copy(high, src[:, :, 2:4, :])
+            low = w1_low[:, :, m_cols, :].rearrange("p t m j -> p m j t")
+            high = w1_high[:, :, m_cols, :].rearrange("p t m j -> p m j t")
+            nc.vector.tensor_copy(low, src[:, :, :, 0:2])
+            nc.scalar.copy(high, src[:, :, :, 2:4])
         w1_codes = keep.tile([P, H], U32, name="w1_codes", align_bytes=64)
         w1_scales = keep.tile([P, H], U8, name="w1_scales", tag="after_first_product", align_bytes=64)
         for t0, t1, grouped in ((0, 1, w1_low[:, 0:1]), (1, 2, w1_low[:, 1:2]), (2, 4, w1_high[:])):
@@ -109,11 +109,12 @@ def tile_picked_permun_relu_p_kernel(tc, x_words, x_scales, w1, w2, offs, back, 
 
         def cast_w2(h):
             grouped = keep.tile([P, w2_width, PACK], BF16, name="w2_grouped%d" % h, tag=("after_w1_quantize", "after_first_product")[h], align_bytes=64)
-            src = w2_raw[:, h].rearrange("p j c -> p c j")
+            src = w2_raw[:, h].rearrange("p j (c i) -> p c j i", i=4)
+            dst = grouped[:].rearrange("p (c i) j -> p c j i", i=4)
             if h == 0:
-                nc.vector.tensor_copy(grouped[:], src)
+                nc.vector.tensor_copy(dst, src)
             else:
-                nc.scalar.copy(grouped[:], src)
+                nc.scalar.copy(dst, src)
             return grouped
 
         def quantize_w2(h, grouped):
@@ -131,15 +132,16 @@ def tile_picked_permun_relu_p_kernel(tc, x_words, x_scales, w1, w2, offs, back, 
 
         def gather_piece(i):
             n, j0 = PIECES[i], starts[i]
-            planes = keep.tile([P, PACK, n], BF16, name="z_planes%d" % i, tag=("z_planes0", "after_relu", "after_z_quantize")[i], align_bytes=64)
+            planes = keep.tile([P, PACK, n], F32, name="z_planes%d" % i, tag=("z_planes0", "after_relu", "after_z_quantize")[i], align_bytes=64)
             for t in range(PACK):
                 nc.vector.tensor_copy(planes[:, t, :], y_planes[t][:].indirect(back_sb[:, j0 // LIST_ROWS : (j0 + n) // LIST_ROWS]))
             grouped = keep.tile([P, n, PACK], BF16, name="z_grouped%d" % i, tag=("after_z_quantize", "z_grouped_late", "z_grouped_late")[i], align_bytes=64)
-            src = planes[:].rearrange("p t n -> p n t")
+            src = planes[:].rearrange("p t (c i) -> p c t i", i=4)
+            dst = grouped[:].rearrange("p (c i) t -> p c t i", i=4)
             if i == last:
-                nc.vector.tensor_copy(grouped[:], src)
+                nc.vector.tensor_copy(dst, src)
             else:
-                nc.scalar.copy(grouped[:], src)
+                nc.scalar.copy(dst, src)
             return grouped
 
         def finish_piece(i, grouped):
@@ -165,7 +167,8 @@ def tile_picked_permun_relu_p_kernel(tc, x_words, x_scales, w1, w2, offs, back, 
                     nc.vector.tensor_copy(staged[:], acc[:])
                 else:
                     nc.scalar.copy(staged[:], acc[:])
-                nc.sync.dma_start(out_rows[:, 2 * half : 2 * half + 2, j0 : j0 + n], staged[:])
+                queue = nc.scalar if i == last and half == 0 else nc.sync
+                queue.dma_start(out_rows[:, 2 * half : 2 * half + 2, j0 : j0 + n], staged[:])
 
         pending = gather_piece(0)
         quantize_w2(1, w2_second)

@@ -17,10 +17,21 @@ RELU = mybir.ActivationFunctionType.Relu
 P = 128
 PACK = 4
 LIST_ROWS = 16
-PIECES = (256, 128, 128)
-W1_CHUNKS = 1
-W2_CHUNKS = 2
+BLOCK_ROWS = 8
+QUADRANT = 32
+LINE = 4
+ALIGN = 64
+BANKS = 8
 WORDS_AHEAD = 512
+PIECES = (256, 128, 128)
+W2_HALF = N // 2
+
+SCALES_THEN_W2 = "scales_then_w2"
+WORDS_THEN_W2_THEN_Z = "words_then_w2_then_z"
+W1_SCALES_THEN_W2 = "w1_scales_then_w2"
+BIAS_THEN_Z = "bias_then_z"
+Z_FIRST_THEN_LAST = "z_first_then_last"
+Z_SECOND_THEN_LAST = "z_second_then_last"
 
 
 def tile_picked_permun_relu_p_kernel(tc, x_words, x_scales, w1, w2, offs, back, out):
@@ -29,151 +40,140 @@ def tile_picked_permun_relu_p_kernel(tc, x_words, x_scales, w1, w2, offs, back, 
         keep = ctx.enter_context(tc.tile_pool(name="keep", bufs=1))
         psum = ctx.enter_context(tc.psum_pool(name="psum", bufs=1))
 
+        def list_slice(list_tile, start, stop):
+            return list_tile[:, start // LIST_ROWS : stop // LIST_ROWS]
+
+        def quantize(codes, scales, values):
+            nc.vector.quantize_mx(out=codes.bitcast(FP8X4), scales=scales, in_=values)
+
+        def multiply(acc, w_codes, w_scales, codes, scales):
+            nc.tensor.matmul_mx(
+                out=acc,
+                lhsT=w_codes.bitcast(FP8X4),
+                lhsT_scale=w_scales,
+                rhs=codes.bitcast(FP8X4),
+                rhs_scale=scales,
+                start=True,
+                stop=True,
+            )
+
+        def interleave(copy, grouped, rows):
+            copy(
+                grouped.rearrange("p (c i) r -> p c r i", i=LINE),
+                rows.rearrange("p r (c i) -> p c r i", i=LINE),
+            )
+
         offs_sb = keep.tile([P, S // LIST_ROWS], U16, name="offs_sb")
         back_sb = keep.tile([P, S // LIST_ROWS], U16, name="back_sb")
-        scale_table = keep.tile([P, T], U8, name="scale_table", tag="after_scale_gather", align_bytes=64)
-
-        word_table = keep.tile([P, T], U32, name="word_table", align_bytes=64)
+        scale_table = keep.tile([P, T], U8, name="scale_table", tag=SCALES_THEN_W2, align_bytes=ALIGN)
+        word_table = keep.tile([P, T], U32, name="word_table", tag=WORDS_THEN_W2_THEN_Z, align_bytes=ALIGN)
         words = x_words[0].rearrange("p n r -> p (n r)").bitcast(I32)
         nc.vector.memset(scale_table[:].bitcast(I32), 0)
         nc.sync.dma_start(offs_sb[:], offs)
         nc.sync.dma_start(word_table[:, :WORDS_AHEAD].bitcast(I32), words[:, :WORDS_AHEAD])
-        nc.sync.dma_start(scale_table[0:P:8, :].bitcast(I32), x_scales[0].bitcast(I32))
-        nc.sync.dma_start(word_table[:, WORDS_AHEAD:].bitcast(I32), words[:, WORDS_AHEAD:])
+        nc.sync.dma_start(scale_table[0:P:BLOCK_ROWS, :].bitcast(I32), x_scales[0].bitcast(I32))
+
         zero_in = keep.tile([P, 1], F32, name="zero_in")
         nc.vector.memset(zero_in[:], 0.0)
-        zero_bias = keep.tile([P, 1], F32, name="zero_bias", tag="after_relu", align_bytes=64)
+        zero_bias = keep.tile([P, 1], F32, name="zero_bias", tag=BIAS_THEN_Z, align_bytes=ALIGN)
         nc.scalar.activation(zero_bias[:], zero_in[:], RELU)
 
-        w1_rows = w1.rearrange("(p j) c -> p j c", j=PACK)
-        w1_width = H // W1_CHUNKS
-        w1_raw = []
-        for h in range(W1_CHUNKS):
-            raw = keep.tile([P, PACK, w1_width], F32, name="w1_raw%d" % h)
-            nc.sync.dma_start(raw[:], w1_rows[:, :, h * w1_width : (h + 1) * w1_width])
-            w1_raw.append(raw)
+        w1_raw = keep.tile([P, PACK, H], F32, name="w1_raw")
+        nc.sync.dma_start(w1_raw[:], w1.rearrange("(p j) c -> p j c", j=PACK))
+        nc.sync.dma_start(word_table[:, WORDS_AHEAD:].bitcast(I32), words[:, WORDS_AHEAD:])
         nc.sync.dma_start(back_sb[:], back)
-        picked_scales = keep.tile([P, S], U8, name="picked_scales", align_bytes=64)
+
+        picked_scales = keep.tile([P, S], U8, name="picked_scales", align_bytes=ALIGN)
         nc.vector.tensor_copy(picked_scales[:], scale_table[:].indirect(offs_sb[:]))
-        x_plane = keep.tile([P, S], U8, name="x_plane", align_bytes=64)
+        x_plane = keep.tile([P, S], U8, name="x_plane", align_bytes=ALIGN)
         nc.vector.memset(x_plane[:].bitcast(I32), 0)
-        for j in range(4):
-            nc.sync.dma_start(x_plane[j:P:32, :].bitcast(I32), picked_scales[8 * j : P : 32, :].bitcast(I32))
+        for row in range(QUADRANT // BLOCK_ROWS):
+            nc.sync.dma_start(
+                x_plane[row:P:QUADRANT, :].bitcast(I32),
+                picked_scales[BLOCK_ROWS * row : P : QUADRANT, :].bitcast(I32),
+            )
+
         w2_rows = w2.rearrange("(p j) c -> p j c", j=PACK)
-        w2_width = N // W2_CHUNKS
-        w2_raw = keep.tile([P, W2_CHUNKS, PACK, w2_width], F32, name="w2_raw", tag="after_scale_gather", align_bytes=64)
-        for h in range(W2_CHUNKS):
-            nc.sync.dma_start(w2_raw[:, h], w2_rows[:, :, h * w2_width : (h + 1) * w2_width])
+        w2_raw = keep.tile([P, 2, PACK, W2_HALF], F32, name="w2_raw", tag=SCALES_THEN_W2, align_bytes=ALIGN)
+        for h in range(2):
+            nc.sync.dma_start(w2_raw[:, h], w2_rows[:, :, h * W2_HALF : (h + 1) * W2_HALF])
 
-
-        x_codes = keep.tile([P, S], U32, name="x_codes", align_bytes=64)
-        nc.vector.tensor_copy(x_codes[:], word_table[:].indirect(offs_sb[:]))
-
-        w1_low = keep.tile([P, 2, P, PACK], BF16, name="w1_low", align_bytes=64)
-        w1_high = keep.tile([P, 2, P, PACK], BF16, name="w1_high", tag="after_w1_quantize", align_bytes=64)
-        m_chunk = w1_width // PACK
-        for h in range(W1_CHUNKS):
-            src = w1_raw[h][:].rearrange("p j (m t) -> p m j t", t=PACK)
-            m_cols = slice(h * m_chunk, (h + 1) * m_chunk)
-            low = w1_low[:, :, m_cols, :].rearrange("p t m j -> p m j t")
-            high = w1_high[:, :, m_cols, :].rearrange("p t m j -> p m j t")
-            nc.vector.tensor_copy(low, src[:, :, :, 0:2])
-            nc.scalar.copy(high, src[:, :, :, 2:4])
-        w1_codes = keep.tile([P, H], U32, name="w1_codes", align_bytes=64)
-        w1_scales = keep.tile([P, H], U8, name="w1_scales", tag="after_first_product", align_bytes=64)
+        w1_low = keep.tile([P, 2, P, PACK], BF16, name="w1_low", align_bytes=ALIGN)
+        w1_high = keep.tile([P, 2, P, PACK], BF16, name="w1_high", align_bytes=ALIGN)
+        w1_dealt = w1_raw[:].rearrange("p j (m t) -> p m j t", t=PACK)
+        nc.vector.tensor_copy(w1_low[:].rearrange("p t m j -> p m j t"), w1_dealt[:, :, :, 0:2])
+        nc.scalar.copy(w1_high[:].rearrange("p t m j -> p m j t"), w1_dealt[:, :, :, 2:4])
+        w1_codes = keep.tile([P, H], U32, name="w1_codes", align_bytes=ALIGN)
+        w1_scales = keep.tile([P, H], U8, name="w1_scales", tag=W1_SCALES_THEN_W2, align_bytes=ALIGN)
         for t0, t1, grouped in ((0, 1, w1_low[:, 0:1]), (1, 2, w1_low[:, 1:2]), (2, 4, w1_high[:])):
-            nc.vector.quantize_mx(
-                out=w1_codes[:, t0 * P : t1 * P].bitcast(FP8X4),
-                scales=w1_scales[:, t0 * P : t1 * P],
-                in_=grouped.rearrange("p t m j -> p (t m j)"),
-            )
+            cols = slice(t0 * P, t1 * P)
+            quantize(w1_codes[:, cols], w1_scales[:, cols], grouped.rearrange("p t m j -> p (t m j)"))
 
-        y_planes = []
-        for t in range(PACK):
-            acc = psum.tile([P, S], F32, name="y_acc%d" % t)
-            nc.tensor.matmul_mx(
-                out=acc[:],
-                lhsT=w1_codes[:, t * P : (t + 1) * P].bitcast(FP8X4),
-                lhsT_scale=w1_scales[:, t * P : (t + 1) * P],
-                rhs=x_codes[:].bitcast(FP8X4),
-                rhs_scale=x_plane[:],
-                start=True,
-                stop=True,
-            )
-            y_plane = keep.tile([P, S], F32, name="y_plane%d" % t)
-            nc.scalar.activation(y_plane[:], acc[:], RELU, bias=zero_bias[:])
-            y_planes.append(y_plane)
+        x_codes = keep.tile([P, S], U32, name="x_codes", align_bytes=ALIGN)
+        first, second, whole = slice(0, S // 2), slice(S // 2, S), slice(0, S)
+        for cols in (first, second):
+            nc.vector.tensor_copy(x_codes[:, cols], word_table[:].indirect(list_slice(offs_sb, cols.start, cols.stop)))
 
-        w2_codes = keep.tile([P, N], U32, name="w2_codes", align_bytes=64)
-        w2_scales = keep.tile([P, N], U8, name="w2_scales", align_bytes=64)
+        y_planes = [keep.tile([P, S], F32, name="y_plane%d" % t) for t in range(PACK)]
+        for t, cols in ((0, first), (1, first), (0, second), (1, second), (2, whole), (3, whole)):
+            y_acc = psum.tile([P, cols.stop - cols.start], F32, name="y_acc", tag="acc", bufs=BANKS)
+            plane = slice(t * P, (t + 1) * P)
+            multiply(y_acc[:], w1_codes[:, plane], w1_scales[:, plane], x_codes[:, cols], x_plane[:, cols])
+            nc.scalar.activation(y_planes[t][:, cols], y_acc[:], RELU, bias=zero_bias[:])
 
-        def cast_w2(h):
-            grouped = keep.tile([P, w2_width, PACK], BF16, name="w2_grouped%d" % h, tag=("after_w1_quantize", "after_first_product")[h], align_bytes=64)
-            src = w2_raw[:, h].rearrange("p j (c i) -> p c j i", i=4)
-            dst = grouped[:].rearrange("p (c i) j -> p c j i", i=4)
-            if h == 0:
-                nc.vector.tensor_copy(dst, src)
-            else:
-                nc.scalar.copy(dst, src)
+        w2_codes = keep.tile([P, N], U32, name="w2_codes", align_bytes=ALIGN)
+        w2_scales = keep.tile([P, N], U8, name="w2_scales", align_bytes=ALIGN)
+
+        def round_w2(h, copy, tag):
+            grouped = keep.tile([P, W2_HALF, PACK], BF16, name="w2_grouped%d" % h, tag=tag, align_bytes=ALIGN)
+            interleave(copy, grouped[:], w2_raw[:, h])
             return grouped
 
         def quantize_w2(h, grouped):
-            cols = slice(h * w2_width, (h + 1) * w2_width)
-            nc.vector.quantize_mx(
-                out=w2_codes[:, cols].bitcast(FP8X4), scales=w2_scales[:, cols], in_=grouped[:].rearrange("p c j -> p (c j)")
-            )
+            cols = slice(h * W2_HALF, (h + 1) * W2_HALF)
+            quantize(w2_codes[:, cols], w2_scales[:, cols], grouped[:].rearrange("p c j -> p (c j)"))
 
-        quantize_w2(0, cast_w2(0))
-        w2_second = cast_w2(1)
+        quantize_w2(0, round_w2(0, nc.vector.tensor_copy, WORDS_THEN_W2_THEN_Z))
+        w2_second = round_w2(1, nc.scalar.copy, W1_SCALES_THEN_W2)
 
         out_rows = out.rearrange("(b p) j -> p b j", p=P)
         starts = [sum(PIECES[:i]) for i in range(len(PIECES))]
         last = len(PIECES) - 1
+        looked_up_tags = (WORDS_THEN_W2_THEN_Z, BIAS_THEN_Z, Z_FIRST_THEN_LAST)
+        grouped_tags = (Z_FIRST_THEN_LAST, Z_SECOND_THEN_LAST, Z_SECOND_THEN_LAST)
 
-        def gather_piece(i):
+        def look_up(i):
             n, j0 = PIECES[i], starts[i]
-            planes = keep.tile([P, PACK, n], F32, name="z_planes%d" % i, tag=("z_planes0", "after_relu", "after_z_quantize")[i], align_bytes=64)
+            looked_up = keep.tile([P, PACK, n], F32, name="z_planes%d" % i, tag=looked_up_tags[i], align_bytes=ALIGN)
             for t in range(PACK):
-                nc.vector.tensor_copy(planes[:, t, :], y_planes[t][:].indirect(back_sb[:, j0 // LIST_ROWS : (j0 + n) // LIST_ROWS]))
-            grouped = keep.tile([P, n, PACK], BF16, name="z_grouped%d" % i, tag=("after_z_quantize", "z_grouped_late", "z_grouped_late")[i], align_bytes=64)
-            src = planes[:].rearrange("p t (c i) -> p c t i", i=4)
-            dst = grouped[:].rearrange("p (c i) t -> p c t i", i=4)
-            if i == last:
-                nc.vector.tensor_copy(dst, src)
-            else:
-                nc.scalar.copy(dst, src)
+                nc.vector.tensor_copy(looked_up[:, t, :], y_planes[t][:].indirect(list_slice(back_sb, j0, j0 + n)))
+            grouped = keep.tile([P, n, PACK], BF16, name="z_grouped%d" % i, tag=grouped_tags[i], align_bytes=ALIGN)
+            interleave(nc.vector.tensor_copy if i == last else nc.scalar.copy, grouped[:], looked_up[:])
             return grouped
 
-        def finish_piece(i, grouped):
+        def finish(i, grouped):
             n, j0 = PIECES[i], starts[i]
-            z_codes = keep.tile([P, n], U32, name="z_codes%d" % i, align_bytes=64)
-            z_scales = keep.tile([P, n], U8, name="z_scales%d" % i, align_bytes=64)
-            nc.vector.quantize_mx(out=z_codes[:].bitcast(FP8X4), scales=z_scales[:], in_=grouped[:].rearrange("p n t -> p (n t)"))
-            for half in range(2):
-                acc = psum.tile([P, 2, n], F32, name="out_acc", tag="out_acc", bufs=4)
-                for b in range(2):
-                    m_cols = slice((2 * half + b) * P, (2 * half + b + 1) * P)
-                    nc.tensor.matmul_mx(
-                        out=acc[:, b, :],
-                        lhsT=w2_codes[:, m_cols].bitcast(FP8X4),
-                        lhsT_scale=w2_scales[:, m_cols],
-                        rhs=z_codes[:].bitcast(FP8X4),
-                        rhs_scale=z_scales[:],
-                        start=True,
-                        stop=True,
-                    )
-                staged = keep.tile([P, 2, n], F32, name="staged%d_%d" % (i, half))
-                if i == last and half == 1:
-                    nc.vector.tensor_copy(staged[:], acc[:])
+            z_codes = keep.tile([P, n], U32, name="z_codes%d" % i, align_bytes=ALIGN)
+            z_scales = keep.tile([P, n], U8, name="z_scales%d" % i, align_bytes=ALIGN)
+            quantize(z_codes[:], z_scales[:], grouped[:].rearrange("p n t -> p (n t)"))
+            blocks = 1 if i == last else 2
+            for b0 in range(0, N // P, blocks):
+                out_acc = psum.tile([P, blocks, n], F32, name="out_acc", tag="acc", bufs=BANKS)
+                for b in range(blocks):
+                    cols = slice((b0 + b) * P, (b0 + b + 1) * P)
+                    multiply(out_acc[:, b, :], w2_codes[:, cols], w2_scales[:, cols], z_codes[:], z_scales[:])
+                staged = keep.tile([P, blocks, n], F32, name="staged%d_%d" % (i, b0))
+                if i == last and b0 % 2 == 1:
+                    nc.vector.tensor_copy(staged[:], out_acc[:])
                 else:
-                    nc.scalar.copy(staged[:], acc[:])
-                queue = nc.scalar if i == last and half == 0 else nc.sync
-                queue.dma_start(out_rows[:, 2 * half : 2 * half + 2, j0 : j0 + n], staged[:])
+                    nc.scalar.copy(staged[:], out_acc[:])
+                queue = nc.scalar if i == last and b0 % 2 == 0 else nc.sync
+                queue.dma_start(out_rows[:, b0 : b0 + blocks, j0 : j0 + n], staged[:])
 
-        pending = gather_piece(0)
+        pending = look_up(0)
         quantize_w2(1, w2_second)
         for i in range(1, len(PIECES)):
-            following = gather_piece(i)
-            finish_piece(i - 1, pending)
+            following = look_up(i)
+            finish(i - 1, pending)
             pending = following
-        finish_piece(last, pending)
+        finish(last, pending)

@@ -24,6 +24,7 @@ ALIGN = 64
 BANKS = 8
 WORDS_AHEAD = 512
 PIECES = (256, 128, 128)
+OWN_PARTS = 2
 W2_HALF = N // 2
 
 SCALES_THEN_W2 = "scales_then_w2"
@@ -57,11 +58,19 @@ def tile_picked_permun_relu_p_kernel(tc, x_words, x_scales, w1, w2, offs, back, 
                 stop=True,
             )
 
-        def interleave(copy, grouped, rows):
-            copy(
-                grouped.rearrange("p (c i) r -> p c r i", i=LINE),
-                rows.rearrange("p r (c i) -> p c r i", i=LINE),
-            )
+        def parts_of(width, parts):
+            return [slice(a, a + width // parts) for a in range(0, width, width // parts)]
+
+        def interleave(copy, grouped, rows, parts):
+            for cols in parts_of(grouped.shape[1], parts):
+                copy(
+                    grouped[:, cols, :].rearrange("p (c i) r -> p c r i", i=LINE),
+                    rows[:, :, cols].rearrange("p r (c i) -> p c r i", i=LINE),
+                )
+
+        def quantize_grouped(codes, scales, grouped, parts):
+            for cols in parts_of(grouped.shape[1], parts):
+                quantize(codes[:, cols], scales[:, cols], grouped[:, cols, :].rearrange("p c r -> p (c r)"))
 
         offs_sb = keep.tile([P, S // LIST_ROWS], U16, name="offs_sb")
         back_sb = keep.tile([P, S // LIST_ROWS], U16, name="back_sb")
@@ -124,17 +133,17 @@ def tile_picked_permun_relu_p_kernel(tc, x_words, x_scales, w1, w2, offs, back, 
         w2_codes = keep.tile([P, N], U32, name="w2_codes", align_bytes=ALIGN)
         w2_scales = keep.tile([P, N], U8, name="w2_scales", align_bytes=ALIGN)
 
-        def round_w2(h, copy, tag):
+        def round_w2(h, copy, tag, parts):
             grouped = keep.tile([P, W2_HALF, PACK], BF16, name="w2_grouped%d" % h, tag=tag, align_bytes=ALIGN)
-            interleave(copy, grouped[:], w2_raw[:, h])
+            interleave(copy, grouped[:], w2_raw[:, h], parts)
             return grouped
 
-        def quantize_w2(h, grouped):
+        def quantize_w2(h, grouped, parts):
             cols = slice(h * W2_HALF, (h + 1) * W2_HALF)
-            quantize(w2_codes[:, cols], w2_scales[:, cols], grouped[:].rearrange("p c j -> p (c j)"))
+            quantize_grouped(w2_codes[:, cols], w2_scales[:, cols], grouped[:], parts)
 
-        quantize_w2(0, round_w2(0, nc.vector.tensor_copy, WORDS_THEN_W2_THEN_Z))
-        w2_second = round_w2(1, nc.scalar.copy, W1_SCALES_THEN_W2)
+        quantize_w2(0, round_w2(0, nc.vector.tensor_copy, WORDS_THEN_W2_THEN_Z, OWN_PARTS), OWN_PARTS)
+        w2_second = round_w2(1, nc.scalar.copy, W1_SCALES_THEN_W2, 1)
 
         out_rows = out.rearrange("(b p) j -> p b j", p=P)
         starts = [sum(PIECES[:i]) for i in range(len(PIECES))]
@@ -148,14 +157,17 @@ def tile_picked_permun_relu_p_kernel(tc, x_words, x_scales, w1, w2, offs, back, 
             for t in range(PACK):
                 nc.vector.tensor_copy(looked_up[:, t, :], y_planes[t][:].indirect(list_slice(back_sb, j0, j0 + n)))
             grouped = keep.tile([P, n, PACK], BF16, name="z_grouped%d" % i, tag=grouped_tags[i], align_bytes=ALIGN)
-            interleave(nc.vector.tensor_copy if i == last else nc.scalar.copy, grouped[:], looked_up[:])
+            if i == last:
+                interleave(nc.vector.tensor_copy, grouped[:], looked_up[:], OWN_PARTS)
+            else:
+                interleave(nc.scalar.copy, grouped[:], looked_up[:], 1)
             return grouped
 
         def finish(i, grouped):
             n, j0 = PIECES[i], starts[i]
             z_codes = keep.tile([P, n], U32, name="z_codes%d" % i, align_bytes=ALIGN)
             z_scales = keep.tile([P, n], U8, name="z_scales%d" % i, align_bytes=ALIGN)
-            quantize(z_codes[:], z_scales[:], grouped[:].rearrange("p n t -> p (n t)"))
+            quantize_grouped(z_codes[:], z_scales[:], grouped[:], OWN_PARTS if i == last else 1)
             blocks = 1 if i == last else 2
             for b0 in range(0, N // P, blocks):
                 out_acc = psum.tile([P, blocks, n], F32, name="out_acc", tag="acc", bufs=BANKS)
@@ -167,11 +179,10 @@ def tile_picked_permun_relu_p_kernel(tc, x_words, x_scales, w1, w2, offs, back, 
                     nc.vector.tensor_copy(staged[:], out_acc[:])
                 else:
                     nc.scalar.copy(staged[:], out_acc[:])
-                queue = nc.scalar if i == last and b0 % 2 == 0 else nc.sync
-                queue.dma_start(out_rows[:, b0 : b0 + blocks, j0 : j0 + n], staged[:])
+                nc.sync.dma_start(out_rows[:, b0 : b0 + blocks, j0 : j0 + n], staged[:])
 
         pending = look_up(0)
-        quantize_w2(1, w2_second)
+        quantize_w2(1, w2_second, 1)
         for i in range(1, len(PIECES)):
             following = look_up(i)
             finish(i - 1, pending)

from contextlib import ExitStack

import concourse.mybir as mybir

K, T, S, N, H = 512, 2048, 512, 512, 512
FLOPS = 2 * K * H * S + 2 * H * N * S

F32 = mybir.dt.float32
BF16 = mybir.dt.bfloat16
I32 = mybir.dt.int32
U32 = mybir.dt.uint32
U16 = mybir.dt.uint16
U8 = mybir.dt.uint8
FP8X4 = mybir.dt.float8_e4m3fn_x4
RELU = mybir.ActivationFunctionType.Relu

P = 128
PACK = 4
LIST_ROWS = 16
BLOCK_ROWS = 8
QUADRANT = 32
LINE = 4
ALIGN = 64
BANKS = 8
WORDS_AHEAD = 512
PIECES = (256, 128, 128)
OWN_PARTS = 2
W2_HALF = N // 2

SCALES_THEN_W2 = "scales_then_w2"
WORDS_THEN_W2_THEN_Z = "words_then_w2_then_z"
W1_SCALES_THEN_W2 = "w1_scales_then_w2"
BIAS_THEN_Z = "bias_then_z"
Z_FIRST_THEN_LAST = "z_first_then_last"
Z_SECOND_THEN_LAST = "z_second_then_last"


def tile_picked_permun_relu_p_kernel(tc, x_words, x_scales, w1, w2, offs, back, out):
    nc = tc.nc
    with ExitStack() as ctx:
        keep = ctx.enter_context(tc.tile_pool(name="keep", bufs=1))
        psum = ctx.enter_context(tc.psum_pool(name="psum", bufs=1))

        def list_slice(list_tile, start, stop):
            return list_tile[:, start // LIST_ROWS : stop // LIST_ROWS]

        def quantize(codes, scales, values):
            nc.vector.quantize_mx(out=codes.bitcast(FP8X4), scales=scales, in_=values)

        def multiply(acc, w_codes, w_scales, codes, scales):
            nc.tensor.matmul_mx(
                out=acc,
                lhsT=w_codes.bitcast(FP8X4),
                lhsT_scale=w_scales,
                rhs=codes.bitcast(FP8X4),
                rhs_scale=scales,
                start=True,
                stop=True,
            )

        def parts_of(width, parts):
            return [slice(a, a + width // parts) for a in range(0, width, width // parts)]

        def interleave(copy, grouped, rows, parts):
            for cols in parts_of(grouped.shape[1], parts):
                copy(
                    grouped[:, cols, :].rearrange("p (c i) r -> p c r i", i=LINE),
                    rows[:, :, cols].rearrange("p r (c i) -> p c r i", i=LINE),
                )

        def quantize_grouped(codes, scales, grouped, parts):
            for cols in parts_of(grouped.shape[1], parts):
                quantize(codes[:, cols], scales[:, cols], grouped[:, cols, :].rearrange("p c r -> p (c r)"))

        offs_sb = keep.tile([P, S // LIST_ROWS], U16, name="offs_sb")
        back_sb = keep.tile([P, S // LIST_ROWS], U16, name="back_sb")
        scale_table = keep.tile([P, T], U8, name="scale_table", tag=SCALES_THEN_W2, align_bytes=ALIGN)
        word_table = keep.tile([P, T], U32, name="word_table", tag=WORDS_THEN_W2_THEN_Z, align_bytes=ALIGN)
        words = x_words[0].rearrange("p n r -> p (n r)").bitcast(I32)
        nc.vector.memset(scale_table[:].bitcast(I32), 0)
        nc.sync.dma_start(offs_sb[:], offs)
        nc.sync.dma_start(word_table[:, :WORDS_AHEAD].bitcast(I32), words[:, :WORDS_AHEAD])
        nc.sync.dma_start(scale_table[0:P:BLOCK_ROWS, :].bitcast(I32), x_scales[0].bitcast(I32))

        zero_in = keep.tile([P, 1], F32, name="zero_in")
        nc.vector.memset(zero_in[:], 0.0)
        zero_bias = keep.tile([P, 1], F32, name="zero_bias", tag=BIAS_THEN_Z, align_bytes=ALIGN)
        nc.scalar.activation(zero_bias[:], zero_in[:], RELU)

        w1_raw = keep.tile([P, PACK, H], F32, name="w1_raw")
        nc.sync.dma_start(w1_raw[:], w1.rearrange("(p j) c -> p j c", j=PACK))
        nc.sync.dma_start(word_table[:, WORDS_AHEAD:].bitcast(I32), words[:, WORDS_AHEAD:])
        nc.sync.dma_start(back_sb[:], back)

        picked_scales = keep.tile([P, S], U8, name="picked_scales", align_bytes=ALIGN)
        nc.vector.tensor_copy(picked_scales[:], scale_table[:].indirect(offs_sb[:]))
        x_plane = keep.tile([P, S], U8, name="x_plane", align_bytes=ALIGN)
        nc.vector.memset(x_plane[:].bitcast(I32), 0)
        for row in range(QUADRANT // BLOCK_ROWS):
            nc.sync.dma_start(
                x_plane[row:P:QUADRANT, :].bitcast(I32),
                picked_scales[BLOCK_ROWS * row : P : QUADRANT, :].bitcast(I32),
            )

        w2_rows = w2.rearrange("(p j) c -> p j c", j=PACK)
        w2_raw = keep.tile([P, 2, PACK, W2_HALF], F32, name="w2_raw", tag=SCALES_THEN_W2, align_bytes=ALIGN)
        for h in range(2):
            nc.sync.dma_start(w2_raw[:, h], w2_rows[:, :, h * W2_HALF : (h + 1) * W2_HALF])

        w1_low = keep.tile([P, 2, P, PACK], BF16, name="w1_low", align_bytes=ALIGN)
        w1_high = keep.tile([P, 2, P, PACK], BF16, name="w1_high", align_bytes=ALIGN)
        w1_dealt = w1_raw[:].rearrange("p j (m t) -> p m j t", t=PACK)
        nc.vector.tensor_copy(w1_low[:].rearrange("p t m j -> p m j t"), w1_dealt[:, :, :, 0:2])
        nc.scalar.copy(w1_high[:].rearrange("p t m j -> p m j t"), w1_dealt[:, :, :, 2:4])
        w1_codes = keep.tile([P, H], U32, name="w1_codes", align_bytes=ALIGN)
        w1_scales = keep.tile([P, H], U8, name="w1_scales", tag=W1_SCALES_THEN_W2, align_bytes=ALIGN)
        for t0, t1, grouped in ((0, 1, w1_low[:, 0:1]), (1, 2, w1_low[:, 1:2]), (2, 4, w1_high[:])):
            cols = slice(t0 * P, t1 * P)
            quantize(w1_codes[:, cols], w1_scales[:, cols], grouped.rearrange("p t m j -> p (t m j)"))

        x_codes = keep.tile([P, S], U32, name="x_codes", align_bytes=ALIGN)
        first, second, whole = slice(0, S // 2), slice(S // 2, S), slice(0, S)
        for cols in (first, second):
            nc.vector.tensor_copy(x_codes[:, cols], word_table[:].indirect(list_slice(offs_sb, cols.start, cols.stop)))

        y_planes = [keep.tile([P, S], F32, name="y_plane%d" % t) for t in range(PACK)]
        for t, cols in ((0, first), (1, first), (0, second), (1, second), (2, whole), (3, whole)):
            y_acc = psum.tile([P, cols.stop - cols.start], F32, name="y_acc", tag="acc", bufs=BANKS)
            plane = slice(t * P, (t + 1) * P)
            multiply(y_acc[:], w1_codes[:, plane], w1_scales[:, plane], x_codes[:, cols], x_plane[:, cols])
            nc.scalar.activation(y_planes[t][:, cols], y_acc[:], RELU, bias=zero_bias[:])

        w2_codes = keep.tile([P, N], U32, name="w2_codes", align_bytes=ALIGN)
        w2_scales = keep.tile([P, N], U8, name="w2_scales", align_bytes=ALIGN)

        def round_w2(h, copy, tag, parts):
            grouped = keep.tile([P, W2_HALF, PACK], BF16, name="w2_grouped%d" % h, tag=tag, align_bytes=ALIGN)
            interleave(copy, grouped[:], w2_raw[:, h], parts)
            return grouped

        def quantize_w2(h, grouped, parts):
            cols = slice(h * W2_HALF, (h + 1) * W2_HALF)
            quantize_grouped(w2_codes[:, cols], w2_scales[:, cols], grouped[:], parts)

        quantize_w2(0, round_w2(0, nc.vector.tensor_copy, WORDS_THEN_W2_THEN_Z, OWN_PARTS), OWN_PARTS)
        w2_second = round_w2(1, nc.scalar.copy, W1_SCALES_THEN_W2, 1)

        out_rows = out.rearrange("(b p) j -> p b j", p=P)
        starts = [sum(PIECES[:i]) for i in range(len(PIECES))]
        last = len(PIECES) - 1
        looked_up_tags = (WORDS_THEN_W2_THEN_Z, BIAS_THEN_Z, Z_FIRST_THEN_LAST)
        grouped_tags = (Z_FIRST_THEN_LAST, Z_SECOND_THEN_LAST, Z_SECOND_THEN_LAST)

        def look_up(i):
            n, j0 = PIECES[i], starts[i]
            looked_up = keep.tile([P, PACK, n], F32, name="z_planes%d" % i, tag=looked_up_tags[i], align_bytes=ALIGN)
            for t in range(PACK):
                nc.vector.tensor_copy(looked_up[:, t, :], y_planes[t][:].indirect(list_slice(back_sb, j0, j0 + n)))
            grouped = keep.tile([P, n, PACK], BF16, name="z_grouped%d" % i, tag=grouped_tags[i], align_bytes=ALIGN)
            if i == last:
                interleave(nc.vector.tensor_copy, grouped[:], looked_up[:], OWN_PARTS)
            else:
                interleave(nc.scalar.copy, grouped[:], looked_up[:], 1)
            return grouped

        def finish(i, grouped):
            n, j0 = PIECES[i], starts[i]
            z_codes = keep.tile([P, n], U32, name="z_codes%d" % i, align_bytes=ALIGN)
            z_scales = keep.tile([P, n], U8, name="z_scales%d" % i, align_bytes=ALIGN)
            quantize_grouped(z_codes[:], z_scales[:], grouped[:], OWN_PARTS if i == last else 1)
            blocks = 1 if i == last else 2
            for b0 in range(0, N // P, blocks):
                out_acc = psum.tile([P, blocks, n], F32, name="out_acc", tag="acc", bufs=BANKS)
                for b in range(blocks):
                    cols = slice((b0 + b) * P, (b0 + b + 1) * P)
                    multiply(out_acc[:, b, :], w2_codes[:, cols], w2_scales[:, cols], z_codes[:], z_scales[:])
                staged = keep.tile([P, blocks, n], F32, name="staged%d_%d" % (i, b0))
                if i == last and b0 % 2 == 1:
                    nc.vector.tensor_copy(staged[:], out_acc[:])
                else:
                    nc.scalar.copy(staged[:], out_acc[:])
                nc.sync.dma_start(out_rows[:, b0 : b0 + blocks, j0 : j0 + n], staged[:])

        pending = look_up(0)
        quantize_w2(1, w2_second, 1)
        for i in range(1, len(PIECES)):
            following = look_up(i)
            finish(i - 1, pending)
            pending = following
        finish(last, pending)
